import numpy as np, ml_dtypes
CORES = [24,40,56,80,88,96]
N = 6
import mx_ref
NC = 256
BF = ml_dtypes.bfloat16
def setup_inputs(rng):
    def f(*shape):
        return mx_ref.flush((rng.standard_normal(shape, dtype=np.float32) * np.exp2(rng.integers(-2, 3, shape[:-1] + (1,)))).astype(BF))
    return {"v": f(N, 128, 512), "p": f(N, 128, N * 4 * NC)}
def setup_inputs_blocks(rng):
    d = setup_inputs(rng)
    for k in ("v", "p"): d[k] = mx_ref.spread(d[k], rng, 2)
    return d
def setup_inputs_wide(rng):
    d = setup_inputs(rng)
    for k in ("v", "p"): d[k] = mx_ref.flush((d[k].astype(np.float32) * np.exp2(rng.integers(-8, 9, (N, 1, 1))).astype(np.float32)).astype(BF))
    return d
def setup_inputs_zeros(rng):
    d = setup_inputs(rng); v = d["p"].reshape(N, 128, -1, 4).copy()
    v[np.broadcast_to((rng.random((N, 1, v.shape[2], 1)) < 0.33), v.shape)] = 0
    d["p"] = v.reshape(d["p"].shape)
    return d
def reference(v, p):
    QV = [mx_ref.quantize(v[j]) for j in range(N)]
    y = np.zeros((N, 128, NC), np.float32)
    for r in range(N):
        for j in range(N):
            s = mx_ref.matmul(QV[j], mx_ref.quantize(p[r][:, 4 * NC * j:4 * NC * j + 4 * NC]))
            y[r] = s if j == 0 else y[r] + s
    return {"y": y}

from concourse.mybir import dt

N = 6
SIM_CORES = 112
VW = 128
PW = 256
FILL = 3

SCRATCH = {
    "vb": ("sbuf", [128, 4 * VW], "bfloat16"),
    "pb": ("sbuf", [128, 4 * PW * N], "bfloat16"),
    "vq": ("sbuf", [128, VW * N], "float8_e4m3fn_x4"),
    "vs": ("sbuf", [128, VW * N], "uint8"),
    "pq": ("sbuf", [128, PW * N], "float8_e4m3fn_x4"),
    "ps": ("sbuf", [128, PW * N], "uint8"),
    "acc": ("psum", [128, 512], "float32"),
    "yb": ("sbuf", [128, PW], "float32"),
}
SEMAPHORES = (["vl", "qv", "gate", "sent", "hin", "mm", "cp", "st"]
              + ["pl%d" % j for j in range(N)] + ["qp%d" % j for j in range(N)] + ["arr%d" % j for j in range(N)])

_CACHE = {}


def _orders(items, k):
    if k == 0:
        return [()]
    return [(x,) + rest for x in items for rest in _orders([y for y in items if y != x], k - 1)]


def _engines(mask):
    return [b for b in range(mask.bit_length()) if (mask >> b) & 1]


def _plan(cores, topo):
    key = tuple(cores)
    if key in _CACHE:
        return _CACHE[key]
    n = len(cores)
    chips = sorted({topo.chip(c) for c in range(SIM_CORES)})

    team = {}
    for c in cores:
        able = [h for h in range(SIM_CORES) if topo.chip(h) == topo.chip(c) and h not in cores
                and all(topo.may_write(h, d) for d in cores if d != c)]
        near = [h for h in able if topo.die(h) == topo.die(c)]
        far = [h for h in able if topo.die(h) != topo.die(c)]
        team[c] = (near[0], near[1], far[0], far[1])

    def way(src, dst):
        a, b, d = topo.chip(src), topo.chip(dst), topo.die(src)
        if a == b:
            return []
        if topo.same_plane(a, b):
            return [("out", a, d), ("in", b, d)]
        if topo.mates(a, b):
            return [("mate", a, d)]
        m = [x for x in chips if topo.mates(a, x)][0]
        return [("mate", a, d), ("out", m, d), ("in", b, d)]

    offs = list(range(1, n))
    k_near = (n - 1) - (n - 1) // 2
    best = None
    for near in _orders(offs, k_near):
        for far in _orders([o for o in offs if o not in near], n - 1 - k_near):
            load, turn = {}, {}
            for i, c in enumerate(cores):
                for group, h in ((near, team[c][0]), (far, team[c][2])):
                    for t, o in enumerate(group):
                        for link in way(h, cores[(i + o) % n]):
                            load[link] = load.get(link, 0) + 1
                            turn[(link, t)] = turn.get((link, t), 0) + 1
            score = (max(load.values()), sum(v - 1 for v in turn.values()), near, far)
            if best is None or score < best:
                best = score
    near, far = best[2], best[3]

    jobs = {}
    for i, c in enumerate(cores):
        for group, hc, hs in ((near, team[c][0], team[c][1]), (far, team[c][2], team[c][3])):
            dests = [cores[(i + o) % n] for o in group]
            jobs[hc] = (i, True, dests)
            jobs[hs] = (i, False, dests)
    arrival = []
    for t in range(k_near):
        arrival += [g[t] for g in (near, far) if t < len(g)]
    via = {}
    for o in near:
        via[o] = 0
    for o in far:
        via[o] = 2
    _CACHE[key] = {"team": team, "jobs": jobs, "arrival": arrival, "via": via}
    return _CACHE[key]


def _tile(T, j, codes):
    if codes:
        return T.vq[:, VW * j:VW * (j + 1)].bitcast(dt.uint8)
    return T.vs[:, VW * j:VW * (j + 1)]


def _send(g, T, topo, dst, j, codes, mask, remote_sem, local_sem):
    rid, pid, _ = topo.addr(dst)
    g.remote_dma(out_ap=_tile(T, j, codes), in_ap=_tile(T, j, codes), remote_sem=remote_sem, local_sem=local_sem,
                 pid=pid, routing_id=rid, dma_engine_mask=mask)


def _halves(mask):
    e = _engines(mask)
    lo, hi = e[:len(e) // 2], e[len(e) // 2:]
    return sum(1 << b for b in lo), sum(1 << b for b in hi)


def rank_program(g, core, T, topo):
    cores = list(T.cores)
    plan = _plan(cores, topo)
    S = T.sem
    rank = T.rank_of(core)

    if rank is None:
        if core not in plan["jobs"]:
            return
        j, codes, dests = plan["jobs"][core]
        a, b = _halves(topo.mask(cores[j], core))
        g.wait_ge(S.hin, len(_engines(a)))
        left = 0
        for d in dests:
            m = topo.mask(core, d)
            _send(g, T, topo, d, j, codes, m, S["arr%d" % j], S.sent)
            left += len(_engines(m))
        g.wait_ge(S.sent, left)
        return

    order = [rank] + [(rank - o) % N for o in plan["arrival"]]

    def pcols(j, w):
        return slice(w * PW * j, w * PW * (j + 1))

    def load(j):
        g.sync.dma_start(T.pb[:, pcols(j, 4)], T.p[:, pcols(j, 4)]).then_inc(S["pl%d" % j], 16)

    hc1, hs1, hc0, hs0 = plan["team"][core]
    m_a, _ = _halves(topo.mask(core, hc1))
    _, m_b = _halves(topo.mask(core, hc0))
    k_a, k_b = len(_engines(m_a)), len(_engines(m_b))

    g.sync.dma_start(T.vb[:], T.v[:]).then_inc(S.vl, 16)
    for j in order[:FILL]:
        load(j)
    g.sync.wait_ge(S.gate, k_b)
    for j in order[FILL:]:
        load(j)

    own = slice(VW * rank, VW * (rank + 1))
    g.vector.wait_ge(S.vl, 16)
    g.vector.quantize_mx(T.vq[:, own], T.vs[:, own], T.vb[:]).then_inc(S.qv, 1)
    for j in order:
        g.vector.wait_ge(S["pl%d" % j], 16)
        g.vector.quantize_mx(T.pq[:, pcols(j, 1)], T.ps[:, pcols(j, 1)], T.pb[:, pcols(j, 4)]).then_inc(S["qp%d" % j], 1)

    g.wait_ge(S.qv, 1)
    _send(g, T, topo, hc1, rank, True, m_a, S.hin, S.sent)
    _send(g, T, topo, hc0, rank, True, m_b, S.hin, S.sent)
    _send(g, T, topo, hs1, rank, False, m_a, S.hin, S.sent)
    _send(g, T, topo, hs0, rank, False, m_b, S.hin, S.gate)
    g.wait_ge(S.sent, 2 * k_a + k_b)

    for k, j in enumerate(order):
        if j == rank:
            g.tensor.wait_ge(S.qv, 1)
        else:
            at = plan["via"][(rank - j) % N]
            pair = plan["team"][cores[j]][at:at + 2]
            g.tensor.wait_ge(S["arr%d" % j], sum(len(_engines(topo.mask(h, core))) for h in pair))
        g.tensor.wait_ge(S["qp%d" % j], 1)
        mm = g.tensor.matmul_mx(T.acc[:, 0:PW], T.vq[:, VW * j:VW * (j + 1)], T.vs[:, VW * j:VW * (j + 1)],
                                T.pq[:, pcols(j, 1)], T.ps[:, pcols(j, 1)], k == 0, k == N - 1)
    mm.then_inc(S.mm, 1)

    g.vector.wait_ge(S.mm, 1)
    g.vector.tensor_copy(T.yb[:], T.acc[:, 0:PW]).then_inc(S.cp, 1)
    g.sync.wait_ge(S.cp, 1)
    g.sync.dma_start(T.y[:], T.yb[:]).then_inc(S.st, 16)
    g.sync.wait_ge(S.st, 16)
